import numpy as np
import ml_dtypes


def mxq(x, axis, fmt="e4m3"):
    dtype, down = {"e4m3": (ml_dtypes.float8_e4m3fn, 7), "e5m2": (ml_dtypes.float8_e5m2, 14)}[fmt]
    v = np.moveaxis(np.asarray(x, np.float32).astype(ml_dtypes.bfloat16).astype(np.float64), axis, -1)
    blocks = v.reshape(v.shape[:-1] + (-1, 32))
    amax = np.abs(blocks).max(-1, keepdims=True)
    byte = np.maximum(np.where(amax > 0, np.frexp(amax)[1] - 1 + 127, 0) - down, 1)
    scale = np.exp2(byte - 127.0)
    codes = (blocks / scale).astype(np.float32).astype(dtype).astype(np.float64)
    return np.moveaxis((codes * scale).reshape(v.shape), -1, axis)


WIDE = False


def mx_kscale(k):
    if not WIDE:
        return np.ones(k)
    levels = np.array([10, -10, 5, -5, 0])
    if k % 512:
        return np.exp2(np.random.permutation(np.resize(levels, k // 32))).repeat(32)
    a = np.empty((k // 512, 16))
    for p in range(k // 512):
        a[p, :8] = np.random.permutation(np.resize(levels, 8))
        for g in range(8):
            far = levels[np.abs(levels - a[p, g]) >= 10]
            a[p, g + 8] = far[np.random.randint(len(far))]
    return np.exp2(a.ravel()).repeat(32)


def f64(x):
    return np.asarray(x).astype(np.float64)


def striped(idx):
    return np.tile(idx.reshape(-1, 16).T, (8, 1)).astype(np.uint16)


def unstriped(offs):
    return offs[:16].T.reshape(-1).astype(np.int64)


E2M1 = np.array([0.0, 0.5, 1.0, 1.5, 2.0, 3.0, 4.0, 6.0, -0.0, -0.5, -1.0, -1.5, -2.0, -3.0, -4.0, -6.0])


def pack_weight(w, fmt):
    k, n = w.shape
    w = f64(np.asarray(w, np.float32).astype(ml_dtypes.bfloat16)).reshape(k // 32, 32, n)
    amax = np.abs(w).max(1)
    if fmt == "e4m3":
        byte = np.frexp(amax)[1] - 1 + 127 - 7
    else:
        mant, ex = np.frexp(amax / 6.0)
        byte = np.where(mant > 0.5, ex, ex - 1) + 127
    byte = np.clip(np.where(amax > 0, byte, 1), 1, 254)
    scaled = (w * np.exp2(127.0 - byte)[:, None, :]).reshape(k, n).astype(np.float32)
    by_word = np.ascontiguousarray(scaled.reshape(k // 512, 128, 4, n).transpose(0, 1, 3, 2))
    if fmt == "e4m3":
        words = by_word.astype(ml_dtypes.float8_e4m3fn).view(np.uint8)
    else:
        c = by_word.astype(ml_dtypes.float4_e2m1fn).view(np.uint8) & 0xF
        words = (c[..., 0::2] | (c[..., 1::2] << 4)).reshape(k // 512, 128, 2 * n)
    return np.ascontiguousarray(words), np.ascontiguousarray(byte.astype(np.uint8).reshape(k // 512, 16, n))


def unpack_weight(words, scales, fmt):
    g, _, n = scales.shape
    words = np.ascontiguousarray(words).reshape(g, 128, n, -1)
    if fmt == "e4m3":
        vals = words.view(ml_dtypes.float8_e4m3fn).astype(np.float64)
    else:
        nib = np.empty((g, 128, n, 4), np.uint8)
        nib[..., 0::2] = words & 0xF
        nib[..., 1::2] = words >> 4
        vals = E2M1[nib]
    vals = vals * np.repeat(np.exp2(scales.astype(np.float64) - 127.0), 8, axis=1)[..., None]
    return vals.transpose(0, 1, 3, 2).reshape(g * 512, n)


def gelu(v):
    return 0.5 * v * (1.0 + np.tanh(np.sqrt(2.0 / np.pi) * (v + 0.044715 * v**3)))


def bf(x):
    return np.asarray(x, np.float32).astype(ml_dtypes.bfloat16)


def planes(Y):
    n, m = Y.shape
    b = f64(bf(Y)).reshape(n // 32, 32, m)
    amax = np.abs(b).max(1)
    byte = np.clip(np.where(amax > 0, np.frexp(amax)[1] - 1 + 127 - 7, 1), 1, 254)
    codes = (b * np.exp2(127.0 - byte)[:, None, :]).reshape(n, m).astype(np.float32).astype(ml_dtypes.float8_e4m3fn).view(np.uint8)
    words = codes.reshape(n // 512, 128, 4, m).transpose(0, 1, 3, 2)
    return np.ascontiguousarray(words), np.ascontiguousarray(byte.astype(np.uint8).reshape(n // 512, 16, m))


K, T, S, H, N = 1024, 2048, 512, 1024, 512

def setup_inputs():
    n = np.random.standard_normal
    s = mx_kscale(K)[:, None]
    u = mx_kscale(H)[:, None]
    tab_words, tab_scales = pack_weight(n((K, T)) * s, "e4m3")
    w2_words, w2_scales = pack_weight(n((K, H)) / np.sqrt(K) / s, "e2m1")
    w3_words, w3_scales = pack_weight(n((K, H)) / np.sqrt(K) / s, "e4m3")
    w4 = n((H, N)) / np.sqrt(H) / u * np.exp(0.8 * n(N))[None, :]
    return {
        "tab_words": tab_words, "tab_scales": tab_scales,
        "offs": striped(np.random.permutation(T)[:S]),
        "offs2": striped(np.random.permutation(T)[:S]),
        "offs3": striped(np.random.permutation(T)[:S]),
        "w1": (1.2 * n((K, H)) / np.sqrt(K) / s).astype(np.float32),
        "w2_words": w2_words, "w2_scales": w2_scales,
        "w3_words": w3_words, "w3_scales": w3_scales,
        "stock": n((H, S)).astype(np.float32),
        "gain": (u[:, 0] * np.exp(0.3 * n(H))).astype(np.float32),
        "w4": w4.astype(np.float32),
    }

def reference(tab_words, tab_scales, offs, offs2, offs3, w1, w2_words, w2_scales,
              w3_words, w3_scales, stock, gain, w4):
    TW = unpack_weight(tab_words, tab_scales, "e4m3")
    v = TW[:, unstriped(offs)]
    v2 = TW[:, unstriped(offs2)]
    v3 = TW[:, unstriped(offs3)]
    bank = mxq(f64(w1), 0, "e4m3").T @ v
    hosp = unpack_weight(w2_words, w2_scales, "e2m1").T @ v2
    route = unpack_weight(w3_words, w3_scales, "e4m3").T @ v3
    st = f64(stock)
    h = f64(gain)[:, None] * (np.tanh(bank + st) * (hosp + st) + route)
    y = mxq(f64(w4), 0, "e4m3").T @ mxq(h, 0, "e4m3")
    words, scales = planes(y)
    return y, words, scales

@@ -1,0 +1,372 @@
+from contextlib import ExitStack
+
+import concourse.mybir as mybir
+
+K, T, S, H, N = 1024, 2048, 512, 1024, 512
+FLOPS = 2 * S * (3 * K * H + H * N)
+
+F32 = mybir.dt.float32
+BF16 = mybir.dt.bfloat16
+I32 = mybir.dt.int32
+U32 = mybir.dt.uint32
+U16 = mybir.dt.uint16
+U8 = mybir.dt.uint8
+FP8X4 = mybir.dt.float8_e4m3fn_x4
+FP4X4 = mybir.dt.float4_e2m1fn_x4
+ADD = mybir.AluOpType.add
+MULT = mybir.AluOpType.mult
+ACT = mybir.ActivationFunctionType
+
+P = 128
+PACK = 4
+KP = P * PACK
+QUADS = 4
+JH = 256
+JC = 128
+CW = 256
+
+
+def tile_list_platelet_route_features_kernel(
+    tc, tab_words, tab_scales, offs, offs2, offs3, w1, w2_words, w2_scales,
+    w3_words, w3_scales, stock, gain, w4, out_0, out_1, out_2,
+):
+    nc = tc.nc
+    with ExitStack() as ctx:
+        keep = ctx.enter_context(tc.tile_pool(name="keep", bufs=1))
+        ring = ctx.enter_context(tc.tile_pool(name="ring", bufs=3))
+        psum = ctx.enter_context(tc.psum_pool(name="psum", bufs=2))
+
+        def held(shape, dtype, name):
+            return keep.tile(shape, dtype, name=name, align_bytes=64)
+
+        lists = [held([P, S // 16], U16, "list%d" % i) for i in range(3)]
+        tab_w = [held([P, T], U32, "tab_w%d" % a) for a in range(2)]
+        tab_s = held([P, T], U8, "tab_s")
+        w_s = held([P, 2 * H], U8, "w_s")
+        w_sd = held([P, 2 * H], U8, "w_sd")
+        v_w = [[held([P, S], U32, "v_w%d%d" % (i, a)) for a in range(2)] for i in range(3)]
+        v_s = [held([P, S], U8, "v_s%d" % i) for i in range(3)]
+        v2_s1 = held([P, S], U8, "v2_s1")
+        w1_raw = {}
+        w4_raw = {}
+        for b in range(2):
+            for hf in range(2):
+                w4_raw[b, hf] = held([P, PACK, CW], F32, "w4_raw%d%d" % (b, hf))
+                for a in range(2):
+                    w1_raw[b, a, hf] = held([P, PACK, CW], F32, "w1_raw%d%d%d" % (b, a, hf))
+        w2_raw = [held([P, 2, 2 * KP], U8, "w2_raw%d" % b) for b in range(2)]
+        w2_d = [held([P, 2 * H], U8, "w2_d%d" % a) for a in range(2)]
+        w3_raw = [held([P, 2, KP], U32, "w3_raw%d" % b) for b in range(2)]
+        w3_d = [held([P, H], U32, "w3_d%d" % a) for a in range(2)]
+        st = [[held([P, PACK, JH], F32, "st%d%d" % (b, jh)) for jh in range(2)] for b in range(2)]
+        g = held([P, 2, PACK], F32, "g")
+
+        nc.vector.memset(tab_s[:].bitcast(I32), 0)
+        nc.gpsimd.memset(w_s[:].bitcast(I32), 0)
+        nc.gpsimd.memset(v2_s1[:].bitcast(I32), 0)
+
+        def load_w1(b, a, hf):
+            rows = w1[a * KP : (a + 1) * KP, b * KP + hf * CW : b * KP + (hf + 1) * CW]
+            nc.sync.dma_start(out=w1_raw[b, a, hf][:], in_=rows.rearrange("(p j) c -> p j c", j=PACK))
+
+        def load_w4(b, hf):
+            rows = w4[b * KP : (b + 1) * KP, hf * CW : (hf + 1) * CW]
+            nc.sync.dma_start(out=w4_raw[b, hf][:], in_=rows.rearrange("(p j) c -> p j c", j=PACK))
+
+        def load_tab(a):
+            nc.sync.dma_start(out=tab_w[a][:].bitcast(I32), in_=tab_words[a].rearrange("p t i -> p (t i)").bitcast(I32))
+
+        def load_wscale(src, row0, q):
+            nc.sync.dma_start(
+                out=w_s[32 * q + row0 : 32 * q + row0 + 4, :].bitcast(I32).rearrange("r (a c) -> r a c", a=2),
+                in_=src[:, 4 * q : 4 * q + 4, :].bitcast(I32).rearrange("a r c -> r a c"),
+            )
+
+        def load_stock(b, jh):
+            rows = stock[b * KP : (b + 1) * KP, jh * JH : (jh + 1) * JH]
+            nc.sync.dma_start(out=st[b][jh][:], in_=rows.rearrange("(p t) j -> p t j", t=PACK))
+
+        def load_w2(b):
+            cols = w2_words[:, :, 2 * b * KP : 2 * (b + 1) * KP].bitcast(I32)
+            nc.sync.dma_start(out=w2_raw[b][:].bitcast(I32), in_=cols.rearrange("a p c -> p a c"))
+
+        def load_w3(b):
+            cols = w3_words.rearrange("a p c i -> a p (c i)")[:, :, 4 * b * KP : 4 * (b + 1) * KP].bitcast(I32)
+            nc.sync.dma_start(out=w3_raw[b][:].bitcast(I32), in_=cols.rearrange("a p c -> p a c"))
+
+        nc.sync.dma_start(lists[1][:], offs2)
+        nc.sync.dma_start(lists[0][:], offs)
+        nc.sync.dma_start(lists[2][:], offs3)
+        for q in range(QUADS):
+            nc.sync.dma_start(
+                out=tab_s[32 * q : 32 * q + 8, :].bitcast(I32),
+                in_=tab_scales[:, 4 * q : 4 * q + 4, :].bitcast(I32),
+            )
+        load_tab(0)
+        for q in range(QUADS):
+            load_w1(0, q // 2, q % 2)
+            load_wscale(w2_scales, 0, q)
+        load_tab(1)
+        load_wscale(w3_scales, 4, 0)
+        load_w2(0)
+        load_wscale(w3_scales, 4, 1)
+        load_w3(0)
+        load_wscale(w3_scales, 4, 2)
+        load_wscale(w3_scales, 4, 3)
+        load_stock(0, 0)
+        nc.sync.dma_start(out=g[:], in_=gain.rearrange("(b p t) -> p b t", b=2, t=PACK))
+        load_w1(1, 0, 0)
+        load_w1(1, 0, 1)
+        load_stock(0, 1)
+        load_w1(1, 1, 0)
+        load_w1(1, 1, 1)
+        load_w2(1)
+        load_w3(1)
+        load_stock(1, 0)
+        load_stock(1, 1)
+        for b in range(2):
+            for hf in range(2):
+                load_w4(b, hf)
+
+        def gather_scales(i):
+            nc.vector.tensor_copy(v_s[i][:], tab_s[:].indirect(lists[i][:]))
+
+        def gather_words(i, a):
+            nc.vector.tensor_copy(v_w[i][a][:], tab_w[a][:].indirect(lists[i][:]))
+
+        def quantize(codes, scales, src):
+            nc.vector.quantize_mx(out=codes.bitcast(FP8X4), scales=scales, in_=src)
+
+        MH = CW // PACK
+
+        def dealt_views(grouped, raw, hf):
+            out = grouped[:].rearrange("p (t m j) -> p m j t", t=PACK, j=PACK)[:, hf * MH : (hf + 1) * MH]
+            return out, raw[:].rearrange("p j (m t) -> p m j t", t=PACK)
+
+        w1_bf = {}
+        w1_c = {}
+        w1_s = {}
+
+        def cast_w1(b, a):
+            w1_bf[b, a] = held([P, PACK * KP], BF16, "w1_bf%d%d" % (b, a))
+            for hf in range(2):
+                out, src = dealt_views(w1_bf[b, a], w1_raw[b, a, hf], hf)
+                nc.scalar.activation(out=out, in_=src, func=ACT.Copy)
+
+        def quant_w1(b, a):
+            w1_c[b, a] = held([P, KP], U32, "w1_c%d%d" % (b, a))
+            w1_s[b, a] = held([P, KP], U8, "w1_s%d%d" % (b, a))
+            quantize(w1_c[b, a][:], w1_s[b, a][:], w1_bf[b, a][:])
+
+        w4_bf = [held([P, PACK * KP], BF16, "w4_bf%d" % b) for b in range(2)]
+        w4_c = [held([P, KP], U32, "w4_c%d" % b) for b in range(2)]
+        w4_s = [held([P, KP], U8, "w4_s%d" % b) for b in range(2)]
+
+        def cast_w4(b):
+            for hf in range(2):
+                out, src = dealt_views(w4_bf[b], w4_raw[b, hf], hf)
+                nc.scalar.activation(out=out, in_=src, func=ACT.Copy)
+
+        def deal(copy, dst, src):
+            copy(out=dst.rearrange("p (t m) -> p m t", t=PACK), in_=src.rearrange("p (m t) -> p m t", t=PACK))
+
+        def deal_scales(b):
+            for a in range(2):
+                cols = slice(a * H + b * KP, a * H + (b + 1) * KP)
+                deal(nc.vector.tensor_copy, w_sd[:, cols], w_s[:, cols])
+
+        def deal_w2(b):
+            for a in range(2):
+                deal(nc.scalar.copy, w2_d[a][:].bitcast(U16)[:, b * KP : (b + 1) * KP], w2_raw[b][:, a, :].bitcast(U16))
+
+        def deal_w3(b):
+            for a in range(2):
+                deal(nc.scalar.copy, w3_d[a][:, b * KP : (b + 1) * KP], w3_raw[b][:, a, :])
+
+        gather_scales(1)
+        for q in range(QUADS):
+            nc.gpsimd.dma_start(
+                out=v2_s1[32 * q : 32 * q + 4, :].bitcast(I32),
+                in_=v_s[1][32 * q + 4 : 32 * q + 8, :].bitcast(I32),
+            )
+        gather_scales(0)
+        gather_scales(2)
+        for i in range(3):
+            gather_words(i, 0)
+        cast_w1(0, 0)
+        cast_w1(0, 1)
+        quant_w1(0, 0)
+        gather_words(0, 1)
+        quant_w1(0, 1)
+        gather_words(1, 1)
+        deal_scales(0)
+        gather_words(2, 1)
+        deal_w2(0)
+        deal_w3(0)
+        deal_scales(1)
+
+        h_bf = {}
+        h_c = [held([P, S], U32, "h_c%d" % b) for b in range(2)]
+        h_s = [held([P, S], U8, "h_s%d" % b) for b in range(2)]
+        y_c = held([P, S], U32, "y_c")
+        y_s = held([P, S], U8, "y_s")
+
+        def product(acc, which, b, jh, u):
+            js = slice(jh * JH, (jh + 1) * JH)
+            for s in range(2):
+                c0 = (2 * u + s) * P
+                for a in range(2):
+                    gc = b * KP + c0
+                    if which == 0:
+                        lhs = w1_c[b, a][:, c0 : c0 + P].bitcast(FP8X4)
+                        lhs_s = w1_s[b, a][:, c0 : c0 + P]
+                        rhs_s = v_s[0][4 * a :, js]
+                    elif which == 1:
+                        lhs = w2_d[a][:, 2 * gc : 2 * gc + 2 * P].bitcast(FP4X4)
+                        lhs_s = w_sd[:, a * H + gc : a * H + gc + P]
+                        rhs_s = (v_s[1] if a == 0 else v2_s1)[:, js]
+                    else:
+                        lhs = w3_d[a][:, gc : gc + P].bitcast(FP8X4)
+                        lhs_s = w_sd[4:, a * H + gc : a * H + gc + P]
+                        rhs_s = v_s[2][4 * a :, js]
+                    nc.tensor.matmul_mx(
+                        out=acc[:, s, :], lhsT=lhs, lhsT_scale=lhs_s,
+                        rhs=v_w[which][a][:, js].bitcast(FP8X4), rhs_scale=rhs_s,
+                        start=(a == 0), stop=(a == 1),
+                    )
+
+        units = [(b, jh, u) for b in range(2) for jh in range(2) for u in range(2)]
+        live = {}
+
+        def front_a(unit):
+            b, jh, u = unit
+            stv = st[b][jh][:, 2 * u : 2 * u + 2, :]
+            bank = psum.tile([P, 2, JH], F32, name="bank")
+            hosp = psum.tile([P, 2, JH], F32, name="hosp")
+            route = psum.tile([P, 2, JH], F32, name="route")
+            product(bank, 0, b, jh, u)
+            product(hosp, 1, b, jh, u)
+            product(route, 2, b, jh, u)
+            pre = ring.tile([P, 2, JH], F32, name="pre")
+            th = ring.tile([P, 2, JH], F32, name="th")
+            nc.vector.tensor_tensor(pre[:], bank[:], stv, ADD)
+            nc.scalar.activation(out=th[:], in_=pre[:], func=ACT.Tanh)
+            live[unit] = [stv, hosp, route, th]
+
+        def front_b(unit):
+            stv, hosp, route, th = live[unit]
+            side = ring.tile([P, 2, JH], F32, name="side")
+            nc.vector.tensor_tensor(side[:], hosp[:], stv, ADD)
+            live[unit] = [side, route, th]
+
+        def back_a(unit):
+            b, jh, u = unit
+            side, route, th = live[unit]
+            prod = ring.tile([P, 2, JH], F32, name="prod")
+            for s in range(2):
+                nc.vector.scalar_tensor_tensor(
+                    prod[:, s, :], th[:, s, :], g[:, b, 2 * u + s : 2 * u + s + 1], side[:, s, :], MULT, MULT)
+            live[unit] = [prod, route]
+
+        def back_b(unit):
+            b, jh, u = unit
+            prod, route = live[unit]
+            if u == 0:
+                h_bf[b, jh] = held([P, PACK, JH], BF16, "h_bf%d%d" % (b, jh))
+            for s in range(2):
+                nc.vector.scalar_tensor_tensor(
+                    h_bf[b, jh][:, 2 * u + s, :], route[:, s, :], g[:, b, 2 * u + s : 2 * u + s + 1],
+                    prod[:, s, :], MULT, ADD)
+
+        def weave(copy, dst, src):
+            copy(
+                out=dst.rearrange("p (c i t) -> p c t i", i=4, t=PACK),
+                in_=src.rearrange("p t (c i) -> p c t i", i=4),
+            )
+
+        def finish_h(b, j0, width, copy):
+            jh, off = divmod(j0, JH)
+            woven = held([P, PACK * width], BF16, "h_wv%d_%d" % (b, j0))
+            weave(copy, woven[:], h_bf[b, jh][:, :, off : off + width])
+            return lambda: quantize(h_c[b][:, j0 : j0 + width], h_s[b][:, j0 : j0 + width], woven[:])
+
+        out_rows = out_0.rearrange("(p t) j -> p t j", t=PACK)
+        out_words = out_1[0].rearrange("p m t -> p (m t)").bitcast(I32)
+
+        def stage2(c, on_vector):
+            js = slice(c * JC, (c + 1) * JC)
+            acc = psum.tile([P, PACK, JC], F32, name="acc")
+            for t in range(PACK):
+                for b in range(2):
+                    nc.tensor.matmul_mx(
+                        out=acc[:, t, :],
+                        lhsT=w4_c[b][:, t * P : (t + 1) * P].bitcast(FP8X4), lhsT_scale=w4_s[b][:, t * P : (t + 1) * P],
+                        rhs=h_c[b][:, js].bitcast(FP8X4), rhs_scale=h_s[b][:, js],
+                        start=(b == 0), stop=(b == 1),
+                    )
+            y = held([P, PACK, JC], F32, "y%d" % c)
+            woven = held([P, PACK * JC], BF16, "y_wv%d" % c)
+            nc.scalar.copy(out=y[:], in_=acc[:])
+            nc.sync.dma_start(out=out_rows[:, :, js], in_=y[:])
+            if on_vector:
+                weave(nc.vector.tensor_copy, woven[:], y[:])
+            else:
+                nc.scalar.copy(out=woven[:].rearrange("p (j t) -> p j t", t=PACK), in_=acc[:].rearrange("p t j -> p j t"))
+            return lambda: quantize(y_c[:, js], y_s[:, js], woven[:])
+
+        def store_words(jh):
+            js = slice(jh * JH, (jh + 1) * JH)
+            nc.sync.dma_start(out=out_words[:, js], in_=y_c[:, js].bitcast(I32))
+
+        pending = []
+        for n in range(len(units) + 1):
+            if n < len(units):
+                front_a(units[n])
+            if n > 0:
+                back_a(units[n - 1])
+            if n < len(units):
+                front_b(units[n])
+            for job in pending:
+                job()
+            pending = []
+            if n > 0:
+                back_b(units[n - 1])
+            if n == 0:
+                cast_w1(1, 0)
+            if n == 1:
+                pending.append(lambda: quant_w1(1, 0))
+                cast_w1(1, 1)
+            if n == 2:
+                pending.append(lambda: quant_w1(1, 1))
+                deal_w2(1)
+                deal_w3(1)
+            if n == 3:
+                pending.append(finish_h(0, 0, JH, nc.scalar.copy))
+            if n == 4:
+                pending.append(finish_h(0, JH, JH, nc.scalar.copy))
+                cast_w4(0)
+            if n == 5:
+                pending.append(lambda: quantize(w4_c[0][:], w4_s[0][:], w4_bf[0][:]))
+                cast_w4(1)
+            if n == 6:
+                pending.append(lambda: quantize(w4_c[1][:], w4_s[1][:], w4_bf[1][:]))
+                pending.append(finish_h(1, 0, JH, nc.scalar.copy))
+            if n == 7:
+                pending.append(stage2(0, False))
+                pending.append(stage2(1, False))
+                pending.append(lambda: store_words(0))
+        q2 = finish_h(1, 2 * JC, JC, nc.vector.tensor_copy)
+        q3 = finish_h(1, 3 * JC, JC, nc.scalar.copy)
+        q2()
+        q3()
+        q2 = stage2(2, True)
+        q3 = stage2(3, True)
+        q2()
+        q3()
+        store_words(1)
+        for q in range(QUADS):
+            queue = nc.sync if q % 2 == 0 else nc.scalar
+            queue.dma_start(
+                out=out_2[0, 4 * q : 4 * q + 4, :].bitcast(I32),
+                in_=y_s[32 * q : 32 * q + 4, :].bitcast(I32),
+            )

@@ -23,7 +23,7 @@ KP = P * PACK
 QUADS = 4
 JH = 256
 JC = 128
-CW = 256
+LINE = 16
 
 
 def tile_list_platelet_route_features_kernel(
@@ -43,48 +43,44 @@ def tile_list_platelet_route_features_kernel(
         tab_w = [held([P, T], U32, "tab_w%d" % a) for a in range(2)]
         tab_s = held([P, T], U8, "tab_s")
         w_s = held([P, 2 * H], U8, "w_s")
-        w_sd = held([P, 2 * H], U8, "w_sd")
+        w_sd = [held([P, 2, KP], U8, "w_sd%d" % b) for b in range(2)]
         v_w = [[held([P, S], U32, "v_w%d%d" % (i, a)) for a in range(2)] for i in range(3)]
         v_s = [held([P, S], U8, "v_s%d" % i) for i in range(3)]
         v2_s1 = held([P, S], U8, "v2_s1")
-        w1_raw = {}
-        w4_raw = {}
-        for b in range(2):
-            for hf in range(2):
-                w4_raw[b, hf] = held([P, PACK, CW], F32, "w4_raw%d%d" % (b, hf))
-                for a in range(2):
-                    w1_raw[b, a, hf] = held([P, PACK, CW], F32, "w1_raw%d%d%d" % (b, a, hf))
+        w1_raw = [[held([P, PACK, KP], F32, "w1_raw%d%d" % (b, a)) for a in range(2)] for b in range(2)]
+        w4_raw = [held([P, PACK, N], F32, "w4_raw%d" % b) for b in range(2)]
         w2_raw = [held([P, 2, 2 * KP], U8, "w2_raw%d" % b) for b in range(2)]
-        w2_d = [held([P, 2 * H], U8, "w2_d%d" % a) for a in range(2)]
+        w2_d = [held([P, 2, 2 * KP], U8, "w2_d%d" % b) for b in range(2)]
         w3_raw = [held([P, 2, KP], U32, "w3_raw%d" % b) for b in range(2)]
-        w3_d = [held([P, H], U32, "w3_d%d" % a) for a in range(2)]
-        st = [[held([P, PACK, JH], F32, "st%d%d" % (b, jh)) for jh in range(2)] for b in range(2)]
+        w3_d = [held([P, 2, KP], U32, "w3_d%d" % b) for b in range(2)]
+        st = [[held([P, 2, S], F32, "st%d%d" % (b, u)) for u in range(2)] for b in range(2)]
         g = held([P, 2, PACK], F32, "g")
 
         nc.vector.memset(tab_s[:].bitcast(I32), 0)
         nc.gpsimd.memset(w_s[:].bitcast(I32), 0)
         nc.gpsimd.memset(v2_s1[:].bitcast(I32), 0)
 
-        def load_w1(b, a, hf):
-            rows = w1[a * KP : (a + 1) * KP, b * KP + hf * CW : b * KP + (hf + 1) * CW]
-            nc.sync.dma_start(out=w1_raw[b, a, hf][:], in_=rows.rearrange("(p j) c -> p j c", j=PACK))
+        def load_w1(b, a):
+            rows = w1[a * KP : (a + 1) * KP, b * KP : (b + 1) * KP]
+            nc.sync.dma_start(out=w1_raw[b][a][:], in_=rows.rearrange("(p j) c -> p j c", j=PACK))
 
-        def load_w4(b, hf):
-            rows = w4[b * KP : (b + 1) * KP, hf * CW : (hf + 1) * CW]
-            nc.sync.dma_start(out=w4_raw[b, hf][:], in_=rows.rearrange("(p j) c -> p j c", j=PACK))
+        def load_w4(b):
+            rows = w4[b * KP : (b + 1) * KP, :]
+            nc.sync.dma_start(out=w4_raw[b][:], in_=rows.rearrange("(p j) c -> p j c", j=PACK))
 
         def load_tab(a):
             nc.sync.dma_start(out=tab_w[a][:].bitcast(I32), in_=tab_words[a].rearrange("p t i -> p (t i)").bitcast(I32))
 
-        def load_wscale(src, row0, q):
-            nc.sync.dma_start(
-                out=w_s[32 * q + row0 : 32 * q + row0 + 4, :].bitcast(I32).rearrange("r (a c) -> r a c", a=2),
-                in_=src[:, 4 * q : 4 * q + 4, :].bitcast(I32).rearrange("a r c -> r a c"),
-            )
+        def load_wscales(src, row0, quads):
+            for q in quads:
+                nc.sync.dma_start(
+                    out=w_s[32 * q + row0 : 32 * q + row0 + 4, :].bitcast(I32).rearrange("r (a c) -> r a c", a=2),
+                    in_=src[:, 4 * q : 4 * q + 4, :].bitcast(I32).rearrange("a r c -> r a c"),
+                )
 
-        def load_stock(b, jh):
-            rows = stock[b * KP : (b + 1) * KP, jh * JH : (jh + 1) * JH]
-            nc.sync.dma_start(out=st[b][jh][:], in_=rows.rearrange("(p t) j -> p t j", t=PACK))
+        def load_stock(b, u):
+            rows = stock[b * KP : (b + 1) * KP, :].rearrange("(p t) j -> p t j", t=PACK)
+            nc.sync.dma_start(out=st[b][u][:], in_=rows[:, 2 * u : 2 * u + 2, :])
 
         def load_w2(b):
             cols = w2_words[:, :, 2 * b * KP : 2 * (b + 1) * KP].bitcast(I32)
@@ -94,6 +90,18 @@ def tile_list_platelet_route_features_kernel(
             cols = w3_words.rearrange("a p c i -> a p (c i)")[:, :, 4 * b * KP : 4 * (b + 1) * KP].bitcast(I32)
             nc.sync.dma_start(out=w3_raw[b][:].bitcast(I32), in_=cols.rearrange("a p c -> p a c"))
 
+        def gather_scales(i):
+            nc.vector.tensor_copy(v_s[i][:], tab_s[:].indirect(lists[i][:]))
+
+        def gather_words(i, a):
+            nc.vector.tensor_copy(v_w[i][a][:], tab_w[a][:].indirect(lists[i][:]))
+
+        def lower_scales(q):
+            nc.sync.dma_start(
+                out=v2_s1[32 * q : 32 * q + 4, :].bitcast(I32),
+                in_=v_s[1][32 * q + 4 : 32 * q + 8, :].bitcast(I32),
+            )
+
         nc.sync.dma_start(lists[1][:], offs2)
         nc.sync.dma_start(lists[0][:], offs)
         nc.sync.dma_start(lists[2][:], offs3)
@@ -102,132 +110,117 @@ def tile_list_platelet_route_features_kernel(
                 out=tab_s[32 * q : 32 * q + 8, :].bitcast(I32),
                 in_=tab_scales[:, 4 * q : 4 * q + 4, :].bitcast(I32),
             )
+        gather_scales(1)
         load_tab(0)
-        for q in range(QUADS):
-            load_w1(0, q // 2, q % 2)
-            load_wscale(w2_scales, 0, q)
+        load_w1(0, 0)
+        load_wscales(w2_scales, 0, (0, 1, 2))
+        load_w1(0, 1)
+        load_wscales(w2_scales, 0, (3,))
+        load_wscales(w3_scales, 4, (0, 1))
         load_tab(1)
-        load_wscale(w3_scales, 4, 0)
+        load_wscales(w3_scales, 4, (2, 3))
         load_w2(0)
-        load_wscale(w3_scales, 4, 1)
+        lower_scales(0)
+        lower_scales(1)
         load_w3(0)
-        load_wscale(w3_scales, 4, 2)
-        load_wscale(w3_scales, 4, 3)
+        lower_scales(2)
+        lower_scales(3)
         load_stock(0, 0)
         nc.sync.dma_start(out=g[:], in_=gain.rearrange("(b p t) -> p b t", b=2, t=PACK))
-        load_w1(1, 0, 0)
-        load_w1(1, 0, 1)
-        load_stock(0, 1)
-        load_w1(1, 1, 0)
-        load_w1(1, 1, 1)
         load_w2(1)
         load_w3(1)
+        load_stock(0, 1)
+        load_w1(1, 0)
+        load_w1(1, 1)
         load_stock(1, 0)
         load_stock(1, 1)
-        for b in range(2):
-            for hf in range(2):
-                load_w4(b, hf)
-
-        def gather_scales(i):
-            nc.vector.tensor_copy(v_s[i][:], tab_s[:].indirect(lists[i][:]))
-
-        def gather_words(i, a):
-            nc.vector.tensor_copy(v_w[i][a][:], tab_w[a][:].indirect(lists[i][:]))
+        load_w4(0)
+        load_w4(1)
 
         def quantize(codes, scales, src):
             nc.vector.quantize_mx(out=codes.bitcast(FP8X4), scales=scales, in_=src)
 
-        MH = CW // PACK
+        def cast_weight(raw, u, name):
+            grouped = held([P, 2 * KP], BF16, name)
+            nc.scalar.activation(
+                out=grouped[:].rearrange("p (t m j) -> p m j t", t=2, j=PACK),
+                in_=raw[:].rearrange("p j (m t) -> p m j t", t=PACK)[:, :, :, 2 * u : 2 * u + 2],
+                func=ACT.Copy,
+            )
+            return grouped
 
-        def dealt_views(grouped, raw, hf):
-            out = grouped[:].rearrange("p (t m j) -> p m j t", t=PACK, j=PACK)[:, hf * MH : (hf + 1) * MH]
-            return out, raw[:].rearrange("p j (m t) -> p m j t", t=PACK)
+        def quant_weight(codes, scales, u, grouped):
+            cols = slice(2 * u * P, 2 * (u + 1) * P)
+            quantize(codes[:, cols], scales[:, cols], grouped[:])
 
-        w1_bf = {}
-        w1_c = {}
-        w1_s = {}
-
-        def cast_w1(b, a):
-            w1_bf[b, a] = held([P, PACK * KP], BF16, "w1_bf%d%d" % (b, a))
-            for hf in range(2):
-                out, src = dealt_views(w1_bf[b, a], w1_raw[b, a, hf], hf)
-                nc.scalar.activation(out=out, in_=src, func=ACT.Copy)
-
-        def quant_w1(b, a):
-            w1_c[b, a] = held([P, KP], U32, "w1_c%d%d" % (b, a))
-            w1_s[b, a] = held([P, KP], U8, "w1_s%d%d" % (b, a))
-            quantize(w1_c[b, a][:], w1_s[b, a][:], w1_bf[b, a][:])
-
-        w4_bf = [held([P, PACK * KP], BF16, "w4_bf%d" % b) for b in range(2)]
+        w1_c = [[held([P, KP], U32, "w1_c%d%d" % (b, a)) for a in range(2)] for b in range(2)]
+        w1_s = [[held([P, KP], U8, "w1_s%d%d" % (b, a)) for a in range(2)] for b in range(2)]
         w4_c = [held([P, KP], U32, "w4_c%d" % b) for b in range(2)]
         w4_s = [held([P, KP], U8, "w4_s%d" % b) for b in range(2)]
 
-        def cast_w4(b):
-            for hf in range(2):
-                out, src = dealt_views(w4_bf[b], w4_raw[b, hf], hf)
-                nc.scalar.activation(out=out, in_=src, func=ACT.Copy)
+        def prep_w1(b, a, u):
+            grouped = cast_weight(w1_raw[b][a], u, "w1_bf%d%d%d" % (b, a, u))
+            return lambda: quant_weight(w1_c[b][a], w1_s[b][a], u, grouped)
 
-        def deal(copy, dst, src):
-            copy(out=dst.rearrange("p (t m) -> p m t", t=PACK), in_=src.rearrange("p (m t) -> p m t", t=PACK))
+        def prep_w4(b, u):
+            grouped = cast_weight(w4_raw[b], u, "w4_bf%d%d" % (b, u))
+            return lambda: quant_weight(w4_c[b], w4_s[b], u, grouped)
+
+        def deal(copy, dst, src, per_line):
+            copy(
+                out=dst.rearrange("p a (t l i) -> p a l t i", t=PACK, i=per_line),
+                in_=src.rearrange("p a (l i t) -> p a l t i", t=PACK, i=per_line),
+            )
 
         def deal_scales(b):
-            for a in range(2):
-                cols = slice(a * H + b * KP, a * H + (b + 1) * KP)
-                deal(nc.vector.tensor_copy, w_sd[:, cols], w_s[:, cols])
+            src = w_s[:].rearrange("p (a c) -> p a c", a=2)[:, :, b * KP : (b + 1) * KP]
+            deal(nc.vector.tensor_copy, w_sd[b][:], src, LINE)
 
         def deal_w2(b):
-            for a in range(2):
-                deal(nc.scalar.copy, w2_d[a][:].bitcast(U16)[:, b * KP : (b + 1) * KP], w2_raw[b][:, a, :].bitcast(U16))
+            deal(nc.scalar.copy, w2_d[b][:].bitcast(U16), w2_raw[b][:].bitcast(U16), LINE // 2)
 
         def deal_w3(b):
-            for a in range(2):
-                deal(nc.scalar.copy, w3_d[a][:, b * KP : (b + 1) * KP], w3_raw[b][:, a, :])
+            deal(nc.scalar.copy, w3_d[b][:], w3_raw[b][:], LINE // 4)
 
-        gather_scales(1)
-        for q in range(QUADS):
-            nc.gpsimd.dma_start(
-                out=v2_s1[32 * q : 32 * q + 4, :].bitcast(I32),
-                in_=v_s[1][32 * q + 4 : 32 * q + 8, :].bitcast(I32),
-            )
         gather_scales(0)
         gather_scales(2)
         for i in range(3):
             gather_words(i, 0)
-        cast_w1(0, 0)
-        cast_w1(0, 1)
-        quant_w1(0, 0)
+        first = [prep_w1(0, a, u) for a in range(2) for u in range(2)]
+        first[0]()
+        first[1]()
         gather_words(0, 1)
-        quant_w1(0, 1)
+        first[2]()
         gather_words(1, 1)
+        first[3]()
         deal_scales(0)
         gather_words(2, 1)
-        deal_w2(0)
-        deal_w3(0)
         deal_scales(1)
+        for b in range(2):
+            deal_w2(b)
+            deal_w3(b)
 
-        h_bf = {}
+        h_bf = [held([P, PACK, S], BF16, "h_bf%d" % b) for b in range(2)]
         h_c = [held([P, S], U32, "h_c%d" % b) for b in range(2)]
         h_s = [held([P, S], U8, "h_s%d" % b) for b in range(2)]
         y_c = held([P, S], U32, "y_c")
         y_s = held([P, S], U8, "y_s")
 
-        def product(acc, which, b, jh, u):
-            js = slice(jh * JH, (jh + 1) * JH)
-            for s in range(2):
-                c0 = (2 * u + s) * P
+        def product(acc, which, b, slots, js):
+            for s, t in enumerate(slots):
+                cols = slice(t * P, (t + 1) * P)
                 for a in range(2):
-                    gc = b * KP + c0
                     if which == 0:
-                        lhs = w1_c[b, a][:, c0 : c0 + P].bitcast(FP8X4)
-                        lhs_s = w1_s[b, a][:, c0 : c0 + P]
+                        lhs = w1_c[b][a][:, cols].bitcast(FP8X4)
+                        lhs_s = w1_s[b][a][:, cols]
                         rhs_s = v_s[0][4 * a :, js]
                     elif which == 1:
-                        lhs = w2_d[a][:, 2 * gc : 2 * gc + 2 * P].bitcast(FP4X4)
-                        lhs_s = w_sd[:, a * H + gc : a * H + gc + P]
+                        lhs = w2_d[b][:, a, 2 * t * P : 2 * (t + 1) * P].bitcast(FP4X4)
+                        lhs_s = w_sd[b][:, a, cols]
                         rhs_s = (v_s[1] if a == 0 else v2_s1)[:, js]
                     else:
-                        lhs = w3_d[a][:, gc : gc + P].bitcast(FP8X4)
-                        lhs_s = w_sd[4:, a * H + gc : a * H + gc + P]
+                        lhs = w3_d[b][:, a, cols].bitcast(FP8X4)
+                        lhs_s = w_sd[b][4:, a, cols]
                         rhs_s = v_s[2][4 * a :, js]
                     nc.tensor.matmul_mx(
                         out=acc[:, s, :], lhsT=lhs, lhsT_scale=lhs_s,
@@ -235,48 +228,48 @@ def tile_list_platelet_route_features_kernel(
                         start=(a == 0), stop=(a == 1),
                     )
 
-        units = [(b, jh, u) for b in range(2) for jh in range(2) for u in range(2)]
+        units = [(0, (t,), 0, S) for t in range(PACK)]
+        units = units + [(1, (2 * u, 2 * u + 1), jh * JH, JH) for jh in range(2) for u in range(2)]
         live = {}
 
         def front_a(unit):
-            b, jh, u = unit
-            stv = st[b][jh][:, 2 * u : 2 * u + 2, :]
-            bank = psum.tile([P, 2, JH], F32, name="bank")
-            hosp = psum.tile([P, 2, JH], F32, name="hosp")
-            route = psum.tile([P, 2, JH], F32, name="route")
-            product(bank, 0, b, jh, u)
-            product(hosp, 1, b, jh, u)
-            product(route, 2, b, jh, u)
-            pre = ring.tile([P, 2, JH], F32, name="pre")
-            th = ring.tile([P, 2, JH], F32, name="th")
+            b, slots, j0, width = unit
+            js = slice(j0, j0 + width)
+            shape = [P, len(slots), width]
+            row = slots[0] % 2
+            stv = st[b][slots[0] // 2][:, row : row + len(slots), js]
+            bank = psum.tile(shape, F32, name="bank")
+            hosp = psum.tile(shape, F32, name="hosp")
+            route = psum.tile(shape, F32, name="route")
+            product(bank, 0, b, slots, js)
+            product(hosp, 1, b, slots, js)
+            product(route, 2, b, slots, js)
+            pre = ring.tile(shape, F32, name="pre")
+            th = ring.tile(shape, F32, name="th")
             nc.vector.tensor_tensor(pre[:], bank[:], stv, ADD)
             nc.scalar.activation(out=th[:], in_=pre[:], func=ACT.Tanh)
-            live[unit] = [stv, hosp, route, th]
+            live[unit] = [shape, stv, hosp, route, th]
 
         def front_b(unit):
-            stv, hosp, route, th = live[unit]
-            side = ring.tile([P, 2, JH], F32, name="side")
+            shape, stv, hosp, route, th = live[unit]
+            side = ring.tile(shape, F32, name="side")
             nc.vector.tensor_tensor(side[:], hosp[:], stv, ADD)
-            live[unit] = [side, route, th]
+            live[unit] = [shape, side, route, th]
 
         def back_a(unit):
-            b, jh, u = unit
-            side, route, th = live[unit]
-            prod = ring.tile([P, 2, JH], F32, name="prod")
-            for s in range(2):
-                nc.vector.scalar_tensor_tensor(
-                    prod[:, s, :], th[:, s, :], g[:, b, 2 * u + s : 2 * u + s + 1], side[:, s, :], MULT, MULT)
+            b, slots, j0, width = unit
+            shape, side, route, th = live[unit]
+            prod = ring.tile(shape, F32, name="prod")
+            for s, t in enumerate(slots):
+                nc.vector.scalar_tensor_tensor(prod[:, s, :], th[:, s, :], g[:, b, t : t + 1], side[:, s, :], MULT, MULT)
             live[unit] = [prod, route]
 
         def back_b(unit):
-            b, jh, u = unit
+            b, slots, j0, width = unit
             prod, route = live[unit]
-            if u == 0:
-                h_bf[b, jh] = held([P, PACK, JH], BF16, "h_bf%d%d" % (b, jh))
-            for s in range(2):
+            for s, t in enumerate(slots):
                 nc.vector.scalar_tensor_tensor(
-                    h_bf[b, jh][:, 2 * u + s, :], route[:, s, :], g[:, b, 2 * u + s : 2 * u + s + 1],
-                    prod[:, s, :], MULT, ADD)
+                    h_bf[b][:, t, j0 : j0 + width], route[:, s, :], g[:, b, t : t + 1], prod[:, s, :], MULT, ADD)
 
         def weave(copy, dst, src):
             copy(
@@ -285,9 +278,8 @@ def tile_list_platelet_route_features_kernel(
             )
 
         def finish_h(b, j0, width, copy):
-            jh, off = divmod(j0, JH)
             woven = held([P, PACK * width], BF16, "h_wv%d_%d" % (b, j0))
-            weave(copy, woven[:], h_bf[b, jh][:, :, off : off + width])
+            weave(copy, woven[:], h_bf[b][:, :, j0 : j0 + width])
             return lambda: quantize(h_c[b][:, j0 : j0 + width], h_s[b][:, j0 : j0 + width], woven[:])
 
         out_rows = out_0.rearrange("(p t) j -> p t j", t=PACK)
@@ -331,30 +323,18 @@ def tile_list_platelet_route_features_kernel(
             pending = []
             if n > 0:
                 back_b(units[n - 1])
-            if n == 0:
-                cast_w1(1, 0)
             if n == 1:
-                pending.append(lambda: quant_w1(1, 0))
-                cast_w1(1, 1)
+                pending = [prep_w1(1, 0, 0), prep_w1(1, 0, 1)]
             if n == 2:
-                pending.append(lambda: quant_w1(1, 1))
-                deal_w2(1)
-                deal_w3(1)
-            if n == 3:
-                pending.append(finish_h(0, 0, JH, nc.scalar.copy))
+                pending = [prep_w1(1, 1, 0), prep_w1(1, 1, 1)]
             if n == 4:
-                pending.append(finish_h(0, JH, JH, nc.scalar.copy))
-                cast_w4(0)
+                pending = [finish_h(0, 0, JH, nc.scalar.copy), prep_w4(0, 0)]
             if n == 5:
-                pending.append(lambda: quantize(w4_c[0][:], w4_s[0][:], w4_bf[0][:]))
-                cast_w4(1)
+                pending = [prep_w4(0, 1), prep_w4(1, 0)]
             if n == 6:
-                pending.append(lambda: quantize(w4_c[1][:], w4_s[1][:], w4_bf[1][:]))
-                pending.append(finish_h(1, 0, JH, nc.scalar.copy))
+                pending = [prep_w4(1, 1), finish_h(1, 0, JH, nc.scalar.copy)]
             if n == 7:
-                pending.append(stage2(0, False))
-                pending.append(stage2(1, False))
-                pending.append(lambda: store_words(0))
+                pending = [finish_h(0, JH, JH, nc.scalar.copy), stage2(0, False), stage2(1, False), lambda: store_words(0)]
         q2 = finish_h(1, 2 * JC, JC, nc.vector.tensor_copy)
         q3 = finish_h(1, 3 * JC, JC, nc.scalar.copy)
         q2()

from contextlib import ExitStack

import concourse.mybir as mybir

K, T, S, H, N = 1024, 2048, 512, 1024, 512
FLOPS = 2 * S * (3 * K * H + H * N)

F32 = mybir.dt.float32
BF16 = mybir.dt.bfloat16
I32 = mybir.dt.int32
U32 = mybir.dt.uint32
U16 = mybir.dt.uint16
U8 = mybir.dt.uint8
FP8X4 = mybir.dt.float8_e4m3fn_x4
FP4X4 = mybir.dt.float4_e2m1fn_x4
ADD = mybir.AluOpType.add
MULT = mybir.AluOpType.mult
ACT = mybir.ActivationFunctionType

P = 128
PACK = 4
KP = P * PACK
QUADS = 4
JH = 256
JC = 128
LINE = 16


def tile_list_platelet_route_features_kernel(
    tc, tab_words, tab_scales, offs, offs2, offs3, w1, w2_words, w2_scales,
    w3_words, w3_scales, stock, gain, w4, out_0, out_1, out_2,
):
    nc = tc.nc
    with ExitStack() as ctx:
        keep = ctx.enter_context(tc.tile_pool(name="keep", bufs=1))
        ring = ctx.enter_context(tc.tile_pool(name="ring", bufs=3))
        psum = ctx.enter_context(tc.psum_pool(name="psum", bufs=2))

        def held(shape, dtype, name):
            return keep.tile(shape, dtype, name=name, align_bytes=64)

        lists = [held([P, S // 16], U16, "list%d" % i) for i in range(3)]
        tab_w = [held([P, T], U32, "tab_w%d" % a) for a in range(2)]
        tab_s = held([P, T], U8, "tab_s")
        w_s = held([P, 2 * H], U8, "w_s")
        w_sd = [held([P, 2, KP], U8, "w_sd%d" % b) for b in range(2)]
        v_w = [[held([P, S], U32, "v_w%d%d" % (i, a)) for a in range(2)] for i in range(3)]
        v_s = [held([P, S], U8, "v_s%d" % i) for i in range(3)]
        v2_s1 = held([P, S], U8, "v2_s1")
        w1_raw = [[held([P, PACK, KP], F32, "w1_raw%d%d" % (b, a)) for a in range(2)] for b in range(2)]
        w4_raw = [held([P, PACK, N], F32, "w4_raw%d" % b) for b in range(2)]
        w2_raw = [held([P, 2, 2 * KP], U8, "w2_raw%d" % b) for b in range(2)]
        w2_d = [held([P, 2, 2 * KP], U8, "w2_d%d" % b) for b in range(2)]
        w3_raw = [held([P, 2, KP], U32, "w3_raw%d" % b) for b in range(2)]
        w3_d = [held([P, 2, KP], U32, "w3_d%d" % b) for b in range(2)]
        st = [[held([P, 2, S], F32, "st%d%d" % (b, u)) for u in range(2)] for b in range(2)]
        g = held([P, 2, PACK], F32, "g")

        nc.vector.memset(tab_s[:].bitcast(I32), 0)
        nc.gpsimd.memset(w_s[:].bitcast(I32), 0)
        nc.gpsimd.memset(v2_s1[:].bitcast(I32), 0)

        def load_w1(b, a):
            rows = w1[a * KP : (a + 1) * KP, b * KP : (b + 1) * KP]
            nc.sync.dma_start(out=w1_raw[b][a][:], in_=rows.rearrange("(p j) c -> p j c", j=PACK))

        def load_w4(b):
            rows = w4[b * KP : (b + 1) * KP, :]
            nc.sync.dma_start(out=w4_raw[b][:], in_=rows.rearrange("(p j) c -> p j c", j=PACK))

        def load_tab(a):
            nc.sync.dma_start(out=tab_w[a][:].bitcast(I32), in_=tab_words[a].rearrange("p t i -> p (t i)").bitcast(I32))

        def load_wscales(src, row0, quads):
            for q in quads:
                nc.sync.dma_start(
                    out=w_s[32 * q + row0 : 32 * q + row0 + 4, :].bitcast(I32).rearrange("r (a c) -> r a c", a=2),
                    in_=src[:, 4 * q : 4 * q + 4, :].bitcast(I32).rearrange("a r c -> r a c"),
                )

        def load_stock(b, u):
            rows = stock[b * KP : (b + 1) * KP, :].rearrange("(p t) j -> p t j", t=PACK)
            nc.sync.dma_start(out=st[b][u][:], in_=rows[:, 2 * u : 2 * u + 2, :])

        def load_w2(b):
            cols = w2_words[:, :, 2 * b * KP : 2 * (b + 1) * KP].bitcast(I32)
            nc.sync.dma_start(out=w2_raw[b][:].bitcast(I32), in_=cols.rearrange("a p c -> p a c"))

        def load_w3(b):
            cols = w3_words.rearrange("a p c i -> a p (c i)")[:, :, 4 * b * KP : 4 * (b + 1) * KP].bitcast(I32)
            nc.sync.dma_start(out=w3_raw[b][:].bitcast(I32), in_=cols.rearrange("a p c -> p a c"))

        def gather_scales(i):
            nc.vector.tensor_copy(v_s[i][:], tab_s[:].indirect(lists[i][:]))

        def gather_words(i, a):
            nc.vector.tensor_copy(v_w[i][a][:], tab_w[a][:].indirect(lists[i][:]))

        def lower_scales(q):
            nc.sync.dma_start(
                out=v2_s1[32 * q : 32 * q + 4, :].bitcast(I32),
                in_=v_s[1][32 * q + 4 : 32 * q + 8, :].bitcast(I32),
            )

        nc.sync.dma_start(lists[1][:], offs2)
        nc.sync.dma_start(lists[0][:], offs)
        nc.sync.dma_start(lists[2][:], offs3)
        for q in range(QUADS):
            nc.sync.dma_start(
                out=tab_s[32 * q : 32 * q + 8, :].bitcast(I32),
                in_=tab_scales[:, 4 * q : 4 * q + 4, :].bitcast(I32),
            )
        gather_scales(1)
        load_tab(0)
        load_w1(0, 0)
        load_wscales(w2_scales, 0, (0, 1, 2))
        load_w1(0, 1)
        load_wscales(w2_scales, 0, (3,))
        load_wscales(w3_scales, 4, (0, 1))
        load_tab(1)
        load_wscales(w3_scales, 4, (2, 3))
        load_w2(0)
        lower_scales(0)
        lower_scales(1)
        load_w3(0)
        lower_scales(2)
        lower_scales(3)
        load_stock(0, 0)
        nc.sync.dma_start(out=g[:], in_=gain.rearrange("(b p t) -> p b t", b=2, t=PACK))
        load_w2(1)
        load_w3(1)
        load_stock(0, 1)
        load_w1(1, 0)
        load_w1(1, 1)
        load_stock(1, 0)
        load_stock(1, 1)
        load_w4(0)
        load_w4(1)

        def quantize(codes, scales, src):
            nc.vector.quantize_mx(out=codes.bitcast(FP8X4), scales=scales, in_=src)

        def cast_weight(raw, u, name):
            grouped = held([P, 2 * KP], BF16, name)
            nc.scalar.activation(
                out=grouped[:].rearrange("p (t m j) -> p m j t", t=2, j=PACK),
                in_=raw[:].rearrange("p j (m t) -> p m j t", t=PACK)[:, :, :, 2 * u : 2 * u + 2],
                func=ACT.Copy,
            )
            return grouped

        def quant_weight(codes, scales, u, grouped):
            cols = slice(2 * u * P, 2 * (u + 1) * P)
            quantize(codes[:, cols], scales[:, cols], grouped[:])

        w1_c = [[held([P, KP], U32, "w1_c%d%d" % (b, a)) for a in range(2)] for b in range(2)]
        w1_s = [[held([P, KP], U8, "w1_s%d%d" % (b, a)) for a in range(2)] for b in range(2)]
        w4_c = [held([P, KP], U32, "w4_c%d" % b) for b in range(2)]
        w4_s = [held([P, KP], U8, "w4_s%d" % b) for b in range(2)]

        def prep_w1(b, a, u):
            grouped = cast_weight(w1_raw[b][a], u, "w1_bf%d%d%d" % (b, a, u))
            return lambda: quant_weight(w1_c[b][a], w1_s[b][a], u, grouped)

        def prep_w4(b, u):
            grouped = cast_weight(w4_raw[b], u, "w4_bf%d%d" % (b, u))
            return lambda: quant_weight(w4_c[b], w4_s[b], u, grouped)

        def deal(copy, dst, src, per_line):
            copy(
                out=dst.rearrange("p a (t l i) -> p a l t i", t=PACK, i=per_line),
                in_=src.rearrange("p a (l i t) -> p a l t i", t=PACK, i=per_line),
            )

        def deal_scales(b):
            src = w_s[:].rearrange("p (a c) -> p a c", a=2)[:, :, b * KP : (b + 1) * KP]
            deal(nc.vector.tensor_copy, w_sd[b][:], src, LINE)

        def deal_w2(b):
            deal(nc.scalar.copy, w2_d[b][:].bitcast(U16), w2_raw[b][:].bitcast(U16), LINE // 2)

        def deal_w3(b):
            deal(nc.scalar.copy, w3_d[b][:], w3_raw[b][:], LINE // 4)

        gather_scales(0)
        gather_scales(2)
        for i in range(3):
            gather_words(i, 0)
        first = [prep_w1(0, a, u) for a in range(2) for u in range(2)]
        first[0]()
        first[1]()
        gather_words(0, 1)
        first[2]()
        gather_words(1, 1)
        first[3]()
        deal_scales(0)
        gather_words(2, 1)
        deal_scales(1)
        for b in range(2):
            deal_w2(b)
            deal_w3(b)

        h_bf = [held([P, PACK, S], BF16, "h_bf%d" % b) for b in range(2)]
        h_c = [held([P, S], U32, "h_c%d" % b) for b in range(2)]
        h_s = [held([P, S], U8, "h_s%d" % b) for b in range(2)]
        y_c = held([P, S], U32, "y_c")
        y_s = held([P, S], U8, "y_s")

        def product(acc, which, b, slots, js):
            for s, t in enumerate(slots):
                cols = slice(t * P, (t + 1) * P)
                for a in range(2):
                    if which == 0:
                        lhs = w1_c[b][a][:, cols].bitcast(FP8X4)
                        lhs_s = w1_s[b][a][:, cols]
                        rhs_s = v_s[0][4 * a :, js]
                    elif which == 1:
                        lhs = w2_d[b][:, a, 2 * t * P : 2 * (t + 1) * P].bitcast(FP4X4)
                        lhs_s = w_sd[b][:, a, cols]
                        rhs_s = (v_s[1] if a == 0 else v2_s1)[:, js]
                    else:
                        lhs = w3_d[b][:, a, cols].bitcast(FP8X4)
                        lhs_s = w_sd[b][4:, a, cols]
                        rhs_s = v_s[2][4 * a :, js]
                    nc.tensor.matmul_mx(
                        out=acc[:, s, :], lhsT=lhs, lhsT_scale=lhs_s,
                        rhs=v_w[which][a][:, js].bitcast(FP8X4), rhs_scale=rhs_s,
                        start=(a == 0), stop=(a == 1),
                    )

        units = [(0, (t,), 0, S) for t in range(PACK)]
        units = units + [(1, (2 * u, 2 * u + 1), jh * JH, JH) for jh in range(2) for u in range(2)]
        live = {}

        def front_a(unit):
            b, slots, j0, width = unit
            js = slice(j0, j0 + width)
            shape = [P, len(slots), width]
            row = slots[0] % 2
            stv = st[b][slots[0] // 2][:, row : row + len(slots), js]
            bank = psum.tile(shape, F32, name="bank")
            hosp = psum.tile(shape, F32, name="hosp")
            route = psum.tile(shape, F32, name="route")
            product(bank, 0, b, slots, js)
            product(hosp, 1, b, slots, js)
            product(route, 2, b, slots, js)
            pre = ring.tile(shape, F32, name="pre")
            th = ring.tile(shape, F32, name="th")
            nc.vector.tensor_tensor(pre[:], bank[:], stv, ADD)
            nc.scalar.activation(out=th[:], in_=pre[:], func=ACT.Tanh)
            live[unit] = [shape, stv, hosp, route, th]

        def front_b(unit):
            shape, stv, hosp, route, th = live[unit]
            side = ring.tile(shape, F32, name="side")
            nc.vector.tensor_tensor(side[:], hosp[:], stv, ADD)
            live[unit] = [shape, side, route, th]

        def back_a(unit):
            b, slots, j0, width = unit
            shape, side, route, th = live[unit]
            prod = ring.tile(shape, F32, name="prod")
            for s, t in enumerate(slots):
                nc.vector.scalar_tensor_tensor(prod[:, s, :], th[:, s, :], g[:, b, t : t + 1], side[:, s, :], MULT, MULT)
            live[unit] = [prod, route]

        def back_b(unit):
            b, slots, j0, width = unit
            prod, route = live[unit]
            for s, t in enumerate(slots):
                nc.vector.scalar_tensor_tensor(
                    h_bf[b][:, t, j0 : j0 + width], route[:, s, :], g[:, b, t : t + 1], prod[:, s, :], MULT, ADD)

        def weave(copy, dst, src):
            copy(
                out=dst.rearrange("p (c i t) -> p c t i", i=4, t=PACK),
                in_=src.rearrange("p t (c i) -> p c t i", i=4),
            )

        def finish_h(b, j0, width, copy):
            woven = held([P, PACK * width], BF16, "h_wv%d_%d" % (b, j0))
            weave(copy, woven[:], h_bf[b][:, :, j0 : j0 + width])
            return lambda: quantize(h_c[b][:, j0 : j0 + width], h_s[b][:, j0 : j0 + width], woven[:])

        out_rows = out_0.rearrange("(p t) j -> p t j", t=PACK)
        out_words = out_1[0].rearrange("p m t -> p (m t)").bitcast(I32)

        def stage2(c, on_vector):
            js = slice(c * JC, (c + 1) * JC)
            acc = psum.tile([P, PACK, JC], F32, name="acc")
            for t in range(PACK):
                for b in range(2):
                    nc.tensor.matmul_mx(
                        out=acc[:, t, :],
                        lhsT=w4_c[b][:, t * P : (t + 1) * P].bitcast(FP8X4), lhsT_scale=w4_s[b][:, t * P : (t + 1) * P],
                        rhs=h_c[b][:, js].bitcast(FP8X4), rhs_scale=h_s[b][:, js],
                        start=(b == 0), stop=(b == 1),
                    )
            y = held([P, PACK, JC], F32, "y%d" % c)
            woven = held([P, PACK * JC], BF16, "y_wv%d" % c)
            nc.scalar.copy(out=y[:], in_=acc[:])
            nc.sync.dma_start(out=out_rows[:, :, js], in_=y[:])
            if on_vector:
                weave(nc.vector.tensor_copy, woven[:], y[:])
            else:
                nc.scalar.copy(out=woven[:].rearrange("p (j t) -> p j t", t=PACK), in_=acc[:].rearrange("p t j -> p j t"))
            return lambda: quantize(y_c[:, js], y_s[:, js], woven[:])

        def store_words(jh):
            js = slice(jh * JH, (jh + 1) * JH)
            nc.sync.dma_start(out=out_words[:, js], in_=y_c[:, js].bitcast(I32))

        pending = []
        for n in range(len(units) + 1):
            if n < len(units):
                front_a(units[n])
            if n > 0:
                back_a(units[n - 1])
            if n < len(units):
                front_b(units[n])
            for job in pending:
                job()
            pending = []
            if n > 0:
                back_b(units[n - 1])
            if n == 1:
                pending = [prep_w1(1, 0, 0), prep_w1(1, 0, 1)]
            if n == 2:
                pending = [prep_w1(1, 1, 0), prep_w1(1, 1, 1)]
            if n == 4:
                pending = [finish_h(0, 0, JH, nc.scalar.copy), prep_w4(0, 0)]
            if n == 5:
                pending = [prep_w4(0, 1), prep_w4(1, 0)]
            if n == 6:
                pending = [prep_w4(1, 1), finish_h(1, 0, JH, nc.scalar.copy)]
            if n == 7:
                pending = [finish_h(0, JH, JH, nc.scalar.copy), stage2(0, False), stage2(1, False), lambda: store_words(0)]
        q2 = finish_h(1, 2 * JC, JC, nc.vector.tensor_copy)
        q3 = finish_h(1, 3 * JC, JC, nc.scalar.copy)
        q2()
        q3()
        q2 = stage2(2, True)
        q3 = stage2(3, True)
        q2()
        q3()
        store_words(1)
        for q in range(QUADS):
            queue = nc.sync if q % 2 == 0 else nc.scalar
            queue.dma_start(
                out=out_2[0, 4 * q : 4 * q + 4, :].bitcast(I32),
                in_=y_s[32 * q : 32 * q + 4, :].bitcast(I32),
            )
